import numpy as np, ml_dtypes
CORES = [71,199,95,223,103,231,111,239,119,247,127,255]
N = 12
R = 64
def setup_inputs(rng):
    m = (rng.standard_normal((N, 128, 128), dtype=np.float32) / 11).astype(ml_dtypes.bfloat16)
    q = rng.standard_normal((128, R), dtype=np.float32).astype(ml_dtypes.bfloat16)
    return {"m": m, "mt": m.transpose(0, 2, 1).copy(), "q": np.broadcast_to(q, (N, 128, R)).copy()}
def setup_inputs_big(rng):
    d = setup_inputs(rng)
    for k in ("m", "mt", "q"): d[k] = (d[k].astype(np.float32) * 1024.0).astype(d[k].dtype)
    return d
def setup_inputs_small(rng):
    d = setup_inputs(rng)
    for k in ("m", "mt", "q"): d[k] = (d[k].astype(np.float32) * (1 / 1024.0)).astype(d[k].dtype)
    return d
def setup_inputs_apart(rng):
    d = setup_inputs(rng)
    f = (10.0 ** rng.permutation(np.linspace(-1.5, 1.5, N))).astype(np.float32).reshape(N, 1, 1)
    for k in ("m", "mt"): d[k] = (d[k].astype(np.float32) * f).astype(d[k].dtype)
    return d
def tie_inputs(x):
    x = dict(x)
    x["mt"] = x["m"].transpose(0, 2, 1).copy(); x["q"] = np.broadcast_to(x["q"][0], x["q"].shape).copy()
    return x
def reference(m, mt, q):
    M, MT, Q = m.astype(np.float64), mt.astype(np.float64), q.astype(np.float64)
    p = sum(MT[j].T @ Q[j] for j in range(N))
    q2 = sum(M[j].T @ p for j in range(N))
    return {"p": np.broadcast_to(p.astype(ml_dtypes.bfloat16 if m.dtype != np.float64 else np.float64), (N, 128, R)), "q2": np.broadcast_to(q2.astype(ml_dtypes.bfloat16 if m.dtype != np.float64 else np.float64), (N, 128, R))}

@@ -1,0 +1,129 @@
+import comms_topo
+from concourse.bass import DstId, RemoteDMATransfer
+
+CORES = [71, 199, 95, 223, 103, 231, 111, 239, 119, 247, 127, 255]
+D = 128
+R = 64
+
+
+def _planes(cores, topo):
+    groups = []
+    for c in cores:
+        for grp in groups:
+            if topo.same_plane(grp[0], c):
+                grp.append(c)
+                break
+        else:
+            groups.append([c])
+    return groups
+
+
+def _partners(groups, topo):
+    a, b = groups
+    pair, free, rest = {}, list(b), []
+    for c in a:
+        m = [d for d in free if topo.mates(c, d)]
+        if m:
+            pair[c], pair[m[0]] = m[0], c
+            free.remove(m[0])
+        else:
+            rest.append(c)
+    for c, d in zip(rest, free):
+        pair[c], pair[d] = d, c
+    return pair
+
+
+_G = _planes(CORES, comms_topo)
+
+SCRATCH = {
+    "gath": ("dram", [max(len(x) for x in _G), D, D], "bfloat16"),
+    "land": ("sbuf", [D, len(_G) * D], "bfloat16"),
+    "q_sb": ("sbuf", [D, R], "bfloat16"),
+    "idsrc": ("sbuf", [D, D + 1], "bfloat16"),
+    "iddram": ("dram", [D + 1, D], "bfloat16"),
+    "ident": ("sbuf", [D, D], "bfloat16"),
+    "st_sb": ("sbuf", [D, D], "bfloat16"),
+    "p_sb": ("sbuf", [D, R], "bfloat16"),
+    "q2_sb": ("sbuf", [D, R], "bfloat16"),
+    "ps_t": ("psum", [D, 512], "float32"),
+    "ps_p": ("psum", [D, 512], "float32"),
+    "ps_q": ("psum", [D, 512], "float32"),
+}
+SEMAPHORES = ["ld_m", "ld_q", "fill", "id1", "id2", "arr1", "arr2", "sent1", "sent2",
+              "mm_t", "cp_t", "mm_p", "cp_p", "mm_q", "cp_q", "st_p", "st_q"]
+
+
+def _send(g, core, topo, dests, srcs, dst_ap, remote_sem, local_sem, alu_op):
+    mask = topo.mask(core, dests[0])
+    ids = []
+    for d in dests:
+        assert topo.may_write(core, d)
+        mask &= topo.mask(core, d)
+        rid, pid = topo.addr(d, core)
+        ids.append(DstId(rid=rid, pnc=pid))
+    g.remote_dma_fused(
+        [RemoteDMATransfer(dst_ids=ids, dma_engine_mask=mask, remote_sem=remote_sem,
+                           srcs=srcs, dsts=[dst_ap for _ in dests], alu_op=alu_op)],
+        local_sem=local_sem)
+    return bin(mask).count("1")
+
+
+def rank_program(g, core, T, topo):
+    if T.rank_of(core) is None:
+        return
+    S = T.sem
+    groups = _planes(list(T.cores), topo)
+    pair = _partners(groups, topo)
+    gi = [k for k, grp in enumerate(groups) if core in grp][0]
+    grp = groups[gi]
+    i, n = grp.index(core), len(grp)
+    nb = len(groups)
+
+    g.sync.dma_start(T.gath[i], T.m[:, :]).then_inc(S.ld_m, 16)
+    g.sync.dma_start(T.q_sb[:, :], T.q[:, :]).then_inc(S.ld_q, 16)
+
+    g.vector.memset(T.idsrc[:, :], 0.0).then_inc(S.fill, 1)
+    g.vector.wait_ge(S.fill, 1)
+    g.vector.memset(T.idsrc[:, 0:1], 1.0).then_inc(S.fill, 1)
+    g.scalar.wait_ge(S.fill, 2)
+    g.scalar.dma_start(T.iddram[:, :], T.idsrc[:, :]).then_inc(S.id1, 16)
+    g.scalar.wait_ge(S.id1, 16)
+    g.scalar.dma_start(T.ident[:, :], T.iddram[0:D, :]).then_inc(S.id2, 16)
+
+    g.wait_ge(S.ld_m, 16)
+    peers = [d for d in grp if d != core]
+    e1 = _send(g, core, topo, peers, [T.gath[i]], T.gath[i], S.arr1, S.sent1, 0)
+
+    g.wait_ge(S.arr1, e1 * len(peers))
+    e2 = _send(g, core, topo, [grp[(i + 1) % n], pair[core]], [T.gath[k] for k in range(n)],
+               T.land[:, gi * D:(gi + 1) * D], S.arr2, S.sent2, 1)
+
+    g.tensor.wait_ge(S.id2, 16)
+    g.tensor.wait_ge(S.arr2, e2 * nb)
+    for u in range(nb):
+        g.tensor.matmul(T.ps_t[:, 0:D], T.land[:, u * D:(u + 1) * D], T.ident[:, :],
+                        u == 0, u == nb - 1).then_inc(S.mm_t, 1)
+    g.vector.wait_ge(S.mm_t, nb)
+    g.vector.tensor_copy(T.st_sb[:, :], T.ps_t[:, 0:D]).then_inc(S.cp_t, 1)
+
+    g.tensor.wait_ge(S.ld_q, 16)
+    g.tensor.wait_ge(S.cp_t, 1)
+    g.tensor.matmul(T.ps_p[:, 0:R], T.st_sb[:, :], T.q_sb[:, :], True, True).then_inc(S.mm_p, 1)
+    g.vector.wait_ge(S.mm_p, 1)
+    g.vector.tensor_copy(T.p_sb[:, :], T.ps_p[:, 0:R]).then_inc(S.cp_p, 1)
+    g.sync.wait_ge(S.cp_p, 1)
+    g.sync.dma_start(T.p[:, :], T.p_sb[:, :]).then_inc(S.st_p, 16)
+
+    g.tensor.wait_ge(S.cp_p, 1)
+    for u in range(nb):
+        g.tensor.matmul(T.ps_q[:, 0:R], T.land[:, u * D:(u + 1) * D], T.p_sb[:, :],
+                        u == 0, u == nb - 1).then_inc(S.mm_q, 1)
+    g.vector.wait_ge(S.mm_q, nb)
+    g.vector.tensor_copy(T.q2_sb[:, :], T.ps_q[:, 0:R]).then_inc(S.cp_q, 1)
+    g.scalar.wait_ge(S.cp_q, 1)
+    g.scalar.dma_start(T.q2[:, :], T.q2_sb[:, :]).then_inc(S.st_q, 16)
+
+    g.wait_ge(S.sent1, e1)
+    g.wait_ge(S.sent2, e2)
+    g.wait_ge(S.st_p, 16)
+    g.wait_ge(S.st_q, 16)

@@ -33,11 +33,20 @@ def _partners(groups, topo):
     return pair
 
 
-_G = _planes(CORES, comms_topo)
+def _quads(cores, topo):
+    groups = _planes(cores, topo)
+    pair = _partners(groups, topo)
+    by_chip = {}
+    for c in groups[0]:
+        by_chip.setdefault(topo.chip(c), []).append(c)
+    return [cs + [pair[c] for c in cs] for cs in by_chip.values()]
+
+
+_Q = _quads(CORES, comms_topo)
 
 SCRATCH = {
-    "gath": ("dram", [max(len(x) for x in _G), D, D], "bfloat16"),
-    "land": ("sbuf", [D, len(_G) * D], "bfloat16"),
+    "raw": ("sbuf", [D, len(_Q[0]) * D], "bfloat16"),
+    "gs": ("sbuf", [D, len(_Q) * D], "bfloat16"),
     "q_sb": ("sbuf", [D, R], "bfloat16"),
     "idsrc": ("sbuf", [D, D + 1], "bfloat16"),
     "iddram": ("dram", [D + 1, D], "bfloat16"),
@@ -45,15 +54,16 @@ SCRATCH = {
     "st_sb": ("sbuf", [D, D], "bfloat16"),
     "p_sb": ("sbuf", [D, R], "bfloat16"),
     "q2_sb": ("sbuf", [D, R], "bfloat16"),
+    "ps_s": ("psum", [D, 512], "float32"),
     "ps_t": ("psum", [D, 512], "float32"),
     "ps_p": ("psum", [D, 512], "float32"),
     "ps_q": ("psum", [D, 512], "float32"),
 }
 SEMAPHORES = ["ld_m", "ld_q", "fill", "id1", "id2", "arr1", "arr2", "sent1", "sent2",
-              "mm_t", "cp_t", "mm_p", "cp_p", "mm_q", "cp_q", "st_p", "st_q"]
+              "mm_s", "cp_s", "mm_t", "cp_t", "mm_p", "cp_p", "mm_q", "cp_q", "st_p", "st_q"]
 
 
-def _send(g, core, topo, dests, srcs, dst_ap, remote_sem, local_sem, alu_op):
+def _send(g, core, topo, dests, ap, remote_sem, local_sem):
     mask = topo.mask(core, dests[0])
     ids = []
     for d in dests:
@@ -63,7 +73,7 @@ def _send(g, core, topo, dests, srcs, dst_ap, remote_sem, local_sem, alu_op):
         ids.append(DstId(rid=rid, pnc=pid))
     g.remote_dma_fused(
         [RemoteDMATransfer(dst_ids=ids, dma_engine_mask=mask, remote_sem=remote_sem,
-                           srcs=srcs, dsts=[dst_ap for _ in dests], alu_op=alu_op)],
+                           srcs=[ap], dsts=[ap for _ in dests], alu_op=0)],
         local_sem=local_sem)
     return bin(mask).count("1")
 
@@ -72,14 +82,19 @@ def rank_program(g, core, T, topo):
     if T.rank_of(core) is None:
         return
     S = T.sem
-    groups = _planes(list(T.cores), topo)
-    pair = _partners(groups, topo)
-    gi = [k for k, grp in enumerate(groups) if core in grp][0]
-    grp = groups[gi]
-    i, n = grp.index(core), len(grp)
-    nb = len(groups)
+    quads = _quads(list(T.cores), topo)
+    k = [x for x, qd in enumerate(quads) if core in qd][0]
+    quad = quads[k]
+    pos, na, nb = quad.index(core), len(quad), len(quads)
+    trio = [qd[pos] for qd in quads]
 
-    g.sync.dma_start(T.gath[i], T.m[:, :]).then_inc(S.ld_m, 16)
+    def raw(j):
+        return T.raw[:, j * D:(j + 1) * D]
+
+    def gs(u):
+        return T.gs[:, u * D:(u + 1) * D]
+
+    g.sync.dma_start(raw(pos), T.m[:, :]).then_inc(S.ld_m, 16)
     g.sync.dma_start(T.q_sb[:, :], T.q[:, :]).then_inc(S.ld_q, 16)
 
     g.vector.memset(T.idsrc[:, :], 0.0).then_inc(S.fill, 1)
@@ -91,18 +106,27 @@ def rank_program(g, core, T, topo):
     g.scalar.dma_start(T.ident[:, :], T.iddram[0:D, :]).then_inc(S.id2, 16)
 
     g.wait_ge(S.ld_m, 16)
-    peers = [d for d in grp if d != core]
-    e1 = _send(g, core, topo, peers, [T.gath[i]], T.gath[i], S.arr1, S.sent1, 0)
-
-    g.wait_ge(S.arr1, e1 * len(peers))
-    e2 = _send(g, core, topo, [grp[(i + 1) % n], pair[core]], [T.gath[k] for k in range(n)],
-               T.land[:, gi * D:(gi + 1) * D], S.arr2, S.sent2, 1)
+    e1 = _send(g, core, topo, [d for d in quad if d != core], raw(pos), S.arr1, S.sent1)
 
     g.tensor.wait_ge(S.id2, 16)
-    g.tensor.wait_ge(S.arr2, e2 * nb)
-    for u in range(nb):
-        g.tensor.matmul(T.ps_t[:, 0:D], T.land[:, u * D:(u + 1) * D], T.ident[:, :],
-                        u == 0, u == nb - 1).then_inc(S.mm_t, 1)
+    g.tensor.wait_ge(S.ld_m, 16)
+    g.tensor.matmul(T.ps_s[:, 0:D], T.ident[:, :], raw(pos), True, False).then_inc(S.mm_s, 1)
+    g.tensor.wait_ge(S.arr1, e1 * (na - 1))
+    others = [j for j in range(na) if j != pos]
+    for j in others:
+        g.tensor.matmul(T.ps_s[:, 0:D], T.ident[:, :], raw(j), False, j == others[-1]).then_inc(S.mm_s, 1)
+    g.vector.wait_ge(S.mm_s, na)
+    g.vector.tensor_copy(gs(k), T.ps_s[:, 0:D]).then_inc(S.cp_s, 1)
+
+    g.wait_ge(S.cp_s, 1)
+    e2 = _send(g, core, topo, [d for d in trio if d != core], gs(k), S.arr2, S.sent2)
+
+    order = [k] + [u for u in range(nb) if u != k]
+    g.tensor.wait_ge(S.cp_s, 1)
+    g.tensor.matmul(T.ps_t[:, 0:D], gs(k), T.ident[:, :], True, False).then_inc(S.mm_t, 1)
+    g.tensor.wait_ge(S.arr2, e2 * (nb - 1))
+    for u in order[1:]:
+        g.tensor.matmul(T.ps_t[:, 0:D], gs(u), T.ident[:, :], False, u == order[-1]).then_inc(S.mm_t, 1)
     g.vector.wait_ge(S.mm_t, nb)
     g.vector.tensor_copy(T.st_sb[:, :], T.ps_t[:, 0:D]).then_inc(S.cp_t, 1)
 
@@ -115,9 +139,8 @@ def rank_program(g, core, T, topo):
     g.sync.dma_start(T.p[:, :], T.p_sb[:, :]).then_inc(S.st_p, 16)
 
     g.tensor.wait_ge(S.cp_p, 1)
-    for u in range(nb):
-        g.tensor.matmul(T.ps_q[:, 0:R], T.land[:, u * D:(u + 1) * D], T.p_sb[:, :],
-                        u == 0, u == nb - 1).then_inc(S.mm_q, 1)
+    for u in order:
+        g.tensor.matmul(T.ps_q[:, 0:R], gs(u), T.p_sb[:, :], u == order[0], u == order[-1]).then_inc(S.mm_q, 1)
     g.vector.wait_ge(S.mm_q, nb)
     g.vector.tensor_copy(T.q2_sb[:, :], T.ps_q[:, 0:R]).then_inc(S.cp_q, 1)
     g.scalar.wait_ge(S.cp_q, 1)

@@ -51,16 +51,16 @@ SCRATCH = {
     "idsrc": ("sbuf", [D, D + 1], "bfloat16"),
     "iddram": ("dram", [D + 1, D], "bfloat16"),
     "ident": ("sbuf", [D, D], "bfloat16"),
-    "st_sb": ("sbuf", [D, D], "bfloat16"),
+    "s_sb": ("sbuf", [D, D], "bfloat16"),
     "p_sb": ("sbuf", [D, R], "bfloat16"),
     "q2_sb": ("sbuf", [D, R], "bfloat16"),
+    "ps_y": ("psum", [D, 512], "float32"),
     "ps_s": ("psum", [D, 512], "float32"),
-    "ps_t": ("psum", [D, 512], "float32"),
     "ps_p": ("psum", [D, 512], "float32"),
     "ps_q": ("psum", [D, 512], "float32"),
 }
 SEMAPHORES = ["ld_m", "ld_q", "fill", "id1", "id2", "arr1", "arr2", "sent1", "sent2",
-              "mm_s", "cp_s", "mm_t", "cp_t", "mm_p", "cp_p", "mm_q", "cp_q", "st_p", "st_q"]
+              "mm_y", "cp_y", "mm_s", "cp_s", "mm_p", "cp_p", "mm_q", "cp_q", "st_p", "st_q"]
 
 
 def _send(g, core, topo, dests, ap, remote_sem, local_sem):
@@ -94,7 +94,7 @@ def rank_program(g, core, T, topo):
     def gs(u):
         return T.gs[:, u * D:(u + 1) * D]
 
-    g.sync.dma_start(raw(pos), T.m[:, :]).then_inc(S.ld_m, 16)
+    g.sync.dma_start(raw(pos), T.mt[:, :]).then_inc(S.ld_m, 16)
     g.sync.dma_start(T.q_sb[:, :], T.q[:, :]).then_inc(S.ld_q, 16)
 
     g.vector.memset(T.idsrc[:, :], 0.0).then_inc(S.fill, 1)
@@ -110,38 +110,38 @@ def rank_program(g, core, T, topo):
 
     g.tensor.wait_ge(S.id2, 16)
     g.tensor.wait_ge(S.ld_m, 16)
-    g.tensor.matmul(T.ps_s[:, 0:D], T.ident[:, :], raw(pos), True, False).then_inc(S.mm_s, 1)
+    g.tensor.matmul(T.ps_y[:, 0:D], T.ident[:, :], raw(pos), True, False).then_inc(S.mm_y, 1)
     g.tensor.wait_ge(S.arr1, e1 * (na - 1))
     others = [j for j in range(na) if j != pos]
     for j in others:
-        g.tensor.matmul(T.ps_s[:, 0:D], T.ident[:, :], raw(j), False, j == others[-1]).then_inc(S.mm_s, 1)
-    g.vector.wait_ge(S.mm_s, na)
-    g.vector.tensor_copy(gs(k), T.ps_s[:, 0:D]).then_inc(S.cp_s, 1)
+        g.tensor.matmul(T.ps_y[:, 0:D], T.ident[:, :], raw(j), False, j == others[-1]).then_inc(S.mm_y, 1)
+    g.vector.wait_ge(S.mm_y, na)
+    g.vector.tensor_copy(gs(k), T.ps_y[:, 0:D]).then_inc(S.cp_y, 1)
 
-    g.wait_ge(S.cp_s, 1)
+    g.wait_ge(S.cp_y, 1)
     e2 = _send(g, core, topo, [d for d in trio if d != core], gs(k), S.arr2, S.sent2)
 
-    order = [k] + [u for u in range(nb) if u != k]
-    g.tensor.wait_ge(S.cp_s, 1)
-    g.tensor.matmul(T.ps_t[:, 0:D], gs(k), T.ident[:, :], True, False).then_inc(S.mm_t, 1)
-    g.tensor.wait_ge(S.arr2, e2 * (nb - 1))
-    for u in order[1:]:
-        g.tensor.matmul(T.ps_t[:, 0:D], gs(u), T.ident[:, :], False, u == order[-1]).then_inc(S.mm_t, 1)
-    g.vector.wait_ge(S.mm_t, nb)
-    g.vector.tensor_copy(T.st_sb[:, :], T.ps_t[:, 0:D]).then_inc(S.cp_t, 1)
-
+    rest = [u for u in range(nb) if u != k]
+    g.tensor.wait_ge(S.cp_y, 1)
     g.tensor.wait_ge(S.ld_q, 16)
-    g.tensor.wait_ge(S.cp_t, 1)
-    g.tensor.matmul(T.ps_p[:, 0:R], T.st_sb[:, :], T.q_sb[:, :], True, True).then_inc(S.mm_p, 1)
-    g.vector.wait_ge(S.mm_p, 1)
+    g.tensor.matmul(T.ps_s[:, 0:D], gs(k), T.ident[:, :], True, False).then_inc(S.mm_s, 1)
+    g.tensor.matmul(T.ps_p[:, 0:R], gs(k), T.q_sb[:, :], True, False).then_inc(S.mm_p, 1)
+    g.tensor.wait_ge(S.arr2, e2 * (nb - 1))
+    for u in rest:
+        g.tensor.matmul(T.ps_s[:, 0:D], gs(u), T.ident[:, :], False, u == rest[-1]).then_inc(S.mm_s, 1)
+    for u in rest:
+        g.tensor.matmul(T.ps_p[:, 0:R], gs(u), T.q_sb[:, :], False, u == rest[-1]).then_inc(S.mm_p, 1)
+    g.vector.wait_ge(S.mm_s, nb)
+    g.vector.tensor_copy(T.s_sb[:, :], T.ps_s[:, 0:D]).then_inc(S.cp_s, 1)
+    g.vector.wait_ge(S.mm_p, nb)
     g.vector.tensor_copy(T.p_sb[:, :], T.ps_p[:, 0:R]).then_inc(S.cp_p, 1)
     g.sync.wait_ge(S.cp_p, 1)
     g.sync.dma_start(T.p[:, :], T.p_sb[:, :]).then_inc(S.st_p, 16)
 
+    g.tensor.wait_ge(S.cp_s, 1)
     g.tensor.wait_ge(S.cp_p, 1)
-    for u in order:
-        g.tensor.matmul(T.ps_q[:, 0:R], gs(u), T.p_sb[:, :], u == order[0], u == order[-1]).then_inc(S.mm_q, 1)
-    g.vector.wait_ge(S.mm_q, nb)
+    g.tensor.matmul(T.ps_q[:, 0:R], T.s_sb[:, :], T.p_sb[:, :], True, True).then_inc(S.mm_q, 1)
+    g.vector.wait_ge(S.mm_q, 1)
     g.vector.tensor_copy(T.q2_sb[:, :], T.ps_q[:, 0:R]).then_inc(S.cp_q, 1)
     g.scalar.wait_ge(S.cp_q, 1)
     g.scalar.dma_start(T.q2[:, :], T.q2_sb[:, :]).then_inc(S.st_q, 16)

@@ -1,5 +1,6 @@
 import comms_topo
 from concourse.bass import DstId, RemoteDMATransfer
+from concourse.mybir import AluOpType
 
 CORES = [71, 199, 95, 223, 103, 231, 111, 239, 119, 247, 127, 255]
 D = 128
@@ -47,20 +48,18 @@ _Q = _quads(CORES, comms_topo)
 SCRATCH = {
     "raw": ("sbuf", [D, len(_Q[0]) * D], "bfloat16"),
     "gs": ("sbuf", [D, len(_Q) * D], "bfloat16"),
-    "q_sb": ("sbuf", [D, R], "bfloat16"),
+    "iq": ("sbuf", [D, D + R], "bfloat16"),
     "idsrc": ("sbuf", [D, D + 1], "bfloat16"),
     "iddram": ("dram", [D + 1, D], "bfloat16"),
-    "ident": ("sbuf", [D, D], "bfloat16"),
-    "s_sb": ("sbuf", [D, D], "bfloat16"),
-    "p_sb": ("sbuf", [D, R], "bfloat16"),
+    "sp_sb": ("sbuf", [D, D + R], "bfloat16"),
     "q2_sb": ("sbuf", [D, R], "bfloat16"),
     "ps_y": ("psum", [D, 512], "float32"),
-    "ps_s": ("psum", [D, 512], "float32"),
-    "ps_p": ("psum", [D, 512], "float32"),
+    "ps_sp": ("psum", [D, 512], "float32"),
     "ps_q": ("psum", [D, 512], "float32"),
 }
-SEMAPHORES = ["ld_m", "ld_q", "fill", "id1", "id2", "arr1", "arr2", "sent1", "sent2",
-              "mm_y", "cp_y", "mm_s", "cp_s", "mm_p", "cp_p", "mm_q", "cp_q", "st_p", "st_q"]
+SEMAPHORES = (["ld_m", "ld_q", "fill", "id1", "id2", "sent1", "sent2",
+               "add_y", "cp_y", "mm_sp", "cp_sp", "mm_q", "cp_q", "st_p", "st_q"]
+              + ["a1_%d" % j for j in range(len(_Q[0]))] + ["a2_%d" % u for u in range(len(_Q))])
 
 
 def _send(g, core, topo, dests, ap, remote_sem, local_sem):
@@ -87,6 +86,7 @@ def rank_program(g, core, T, topo):
     quad = quads[k]
     pos, na, nb = quad.index(core), len(quad), len(quads)
     trio = [qd[pos] for qd in quads]
+    ident = T.iq[:, 0:D]
 
     def raw(j):
         return T.raw[:, j * D:(j + 1) * D]
@@ -95,7 +95,7 @@ def rank_program(g, core, T, topo):
         return T.gs[:, u * D:(u + 1) * D]
 
     g.sync.dma_start(raw(pos), T.mt[:, :]).then_inc(S.ld_m, 16)
-    g.sync.dma_start(T.q_sb[:, :], T.q[:, :]).then_inc(S.ld_q, 16)
+    g.sync.dma_start(T.iq[:, D:D + R], T.q[:, :]).then_inc(S.ld_q, 16)
 
     g.vector.memset(T.idsrc[:, :], 0.0).then_inc(S.fill, 1)
     g.vector.wait_ge(S.fill, 1)
@@ -103,44 +103,43 @@ def rank_program(g, core, T, topo):
     g.scalar.wait_ge(S.fill, 2)
     g.scalar.dma_start(T.iddram[:, :], T.idsrc[:, :]).then_inc(S.id1, 16)
     g.scalar.wait_ge(S.id1, 16)
-    g.scalar.dma_start(T.ident[:, :], T.iddram[0:D, :]).then_inc(S.id2, 16)
+    g.scalar.dma_start(ident, T.iddram[0:D, :]).then_inc(S.id2, 16)
 
     g.wait_ge(S.ld_m, 16)
-    e1 = _send(g, core, topo, [d for d in quad if d != core], raw(pos), S.arr1, S.sent1)
+    e1 = _send(g, core, topo, [quad[(pos + t) % na] for t in range(1, na)], raw(pos), S["a1_%d" % pos], S.sent1)
 
-    g.tensor.wait_ge(S.id2, 16)
-    g.tensor.wait_ge(S.ld_m, 16)
-    g.tensor.matmul(T.ps_y[:, 0:D], T.ident[:, :], raw(pos), True, False).then_inc(S.mm_y, 1)
-    g.tensor.wait_ge(S.arr1, e1 * (na - 1))
-    others = [j for j in range(na) if j != pos]
-    for j in others:
-        g.tensor.matmul(T.ps_y[:, 0:D], T.ident[:, :], raw(j), False, j == others[-1]).then_inc(S.mm_y, 1)
-    g.vector.wait_ge(S.mm_y, na)
-    g.vector.tensor_copy(gs(k), T.ps_y[:, 0:D]).then_inc(S.cp_y, 1)
+    g.vector.wait_ge(S.ld_m, 16)
+    acc = raw(pos)
+    for t in range(1, na):
+        j = (pos - t) % na
+        g.vector.wait_ge(S["a1_%d" % j], e1)
+        if t > 1:
+            g.vector.wait_ge(S.add_y, t - 1)
+        if t < na - 1:
+            out = T.ps_y[:, (t - 1) * D:t * D]
+            g.vector.tensor_tensor(out, acc, raw(j), AluOpType.add).then_inc(S.add_y, 1)
+            acc = out
+        else:
+            g.vector.tensor_tensor(gs(k), acc, raw(j), AluOpType.add).then_inc(S.cp_y, 1)
 
     g.wait_ge(S.cp_y, 1)
-    e2 = _send(g, core, topo, [d for d in trio if d != core], gs(k), S.arr2, S.sent2)
+    e2 = _send(g, core, topo, [trio[(k + t) % nb] for t in range(1, nb)], gs(k), S["a2_%d" % k], S.sent2)
 
-    rest = [u for u in range(nb) if u != k]
-    g.tensor.wait_ge(S.cp_y, 1)
+    g.tensor.wait_ge(S.id2, 16)
     g.tensor.wait_ge(S.ld_q, 16)
-    g.tensor.matmul(T.ps_s[:, 0:D], gs(k), T.ident[:, :], True, False).then_inc(S.mm_s, 1)
-    g.tensor.matmul(T.ps_p[:, 0:R], gs(k), T.q_sb[:, :], True, False).then_inc(S.mm_p, 1)
-    g.tensor.wait_ge(S.arr2, e2 * (nb - 1))
-    for u in rest:
-        g.tensor.matmul(T.ps_s[:, 0:D], gs(u), T.ident[:, :], False, u == rest[-1]).then_inc(S.mm_s, 1)
-    for u in rest:
-        g.tensor.matmul(T.ps_p[:, 0:R], gs(u), T.q_sb[:, :], False, u == rest[-1]).then_inc(S.mm_p, 1)
-    g.vector.wait_ge(S.mm_s, nb)
-    g.vector.tensor_copy(T.s_sb[:, :], T.ps_s[:, 0:D]).then_inc(S.cp_s, 1)
-    g.vector.wait_ge(S.mm_p, nb)
-    g.vector.tensor_copy(T.p_sb[:, :], T.ps_p[:, 0:R]).then_inc(S.cp_p, 1)
-    g.sync.wait_ge(S.cp_p, 1)
-    g.sync.dma_start(T.p[:, :], T.p_sb[:, :]).then_inc(S.st_p, 16)
+    g.tensor.wait_ge(S.cp_y, 1)
+    g.tensor.matmul(T.ps_sp[:, 0:D + R], gs(k), T.iq[:, :], True, False).then_inc(S.mm_sp, 1)
+    for t in range(1, nb):
+        u = (k - t) % nb
+        g.tensor.wait_ge(S["a2_%d" % u], e2)
+        g.tensor.matmul(T.ps_sp[:, 0:D + R], gs(u), T.iq[:, :], False, t == nb - 1).then_inc(S.mm_sp, 1)
+    g.vector.wait_ge(S.mm_sp, nb)
+    g.vector.tensor_copy(T.sp_sb[:, :], T.ps_sp[:, 0:D + R]).then_inc(S.cp_sp, 1)
+    g.sync.wait_ge(S.cp_sp, 1)
+    g.sync.dma_start(T.p[:, :], T.sp_sb[:, D:D + R]).then_inc(S.st_p, 16)
 
-    g.tensor.wait_ge(S.cp_s, 1)
-    g.tensor.wait_ge(S.cp_p, 1)
-    g.tensor.matmul(T.ps_q[:, 0:R], T.s_sb[:, :], T.p_sb[:, :], True, True).then_inc(S.mm_q, 1)
+    g.tensor.wait_ge(S.cp_sp, 1)
+    g.tensor.matmul(T.ps_q[:, 0:R], T.sp_sb[:, 0:D], T.sp_sb[:, D:D + R], True, True).then_inc(S.mm_q, 1)
     g.vector.wait_ge(S.mm_q, 1)
     g.vector.tensor_copy(T.q2_sb[:, :], T.ps_q[:, 0:R]).then_inc(S.cp_q, 1)
     g.scalar.wait_ge(S.cp_q, 1)

@@ -1,65 +1,41 @@
 import comms_topo
 from concourse.bass import DstId, RemoteDMATransfer
-from concourse.mybir import AluOpType
+from concourse.mybir import AluOpType, ActivationFunctionType
 
 CORES = [71, 199, 95, 223, 103, 231, 111, 239, 119, 247, 127, 255]
+N = len(CORES)
 D = 128
 R = 64
 
+SCRATCH = {
+    "raw": ("sbuf", [D, N * D], "bfloat16"),
+    "gs": ("sbuf", [D, N * D], "bfloat16"),
+    "ones": ("sbuf", [D, D], "bfloat16"),
+    "ident": ("sbuf", [D, D], "bfloat16"),
+    "q_sb": ("sbuf", [D, R], "bfloat16"),
+    "s_sb": ("sbuf", [D, D], "bfloat16"),
+    "p_sb": ("sbuf", [D, R], "bfloat16"),
+    "q2_sb": ("sbuf", [D, R], "bfloat16"),
+    "ps_y": ("psum", [D, 512], "float32"),
+    "ps_s": ("psum", [D, 512], "float32"),
+    "ps_p": ("psum", [D, 512], "float32"),
+    "ps_q": ("psum", [D, 512], "float32"),
+}
+SEMAPHORES = (["ld_m", "ld_q", "fill", "made_i", "sent", "add_y", "cp_y",
+               "mm_s", "mm_p", "cp_s", "cp_p", "mm_q", "cp_q", "st_p", "st_q"]
+              + ["a_%d" % j for j in range(N)] + ["b_%d" % j for j in range(N)])
 
-def _planes(cores, topo):
+
+def _groups(cores, topo):
     groups = []
     for c in cores:
         for grp in groups:
-            if topo.same_plane(grp[0], c):
+            if topo.same_plane(grp[0], c) and topo.host(grp[0]) == topo.host(c):
                 grp.append(c)
                 break
         else:
             groups.append([c])
-    return groups
-
-
-def _partners(groups, topo):
-    a, b = groups
-    pair, free, rest = {}, list(b), []
-    for c in a:
-        m = [d for d in free if topo.mates(c, d)]
-        if m:
-            pair[c], pair[m[0]] = m[0], c
-            free.remove(m[0])
-        else:
-            rest.append(c)
-    for c, d in zip(rest, free):
-        pair[c], pair[d] = d, c
-    return pair
-
-
-def _quads(cores, topo):
-    groups = _planes(cores, topo)
-    pair = _partners(groups, topo)
-    by_chip = {}
-    for c in groups[0]:
-        by_chip.setdefault(topo.chip(c), []).append(c)
-    return [cs + [pair[c] for c in cs] for cs in by_chip.values()]
-
-
-_Q = _quads(CORES, comms_topo)
-
-SCRATCH = {
-    "raw": ("sbuf", [D, len(_Q[0]) * D], "bfloat16"),
-    "gs": ("sbuf", [D, len(_Q) * D], "bfloat16"),
-    "iq": ("sbuf", [D, D + R], "bfloat16"),
-    "idsrc": ("sbuf", [D, D + 1], "bfloat16"),
-    "iddram": ("dram", [D + 1, D], "bfloat16"),
-    "sp_sb": ("sbuf", [D, D + R], "bfloat16"),
-    "q2_sb": ("sbuf", [D, R], "bfloat16"),
-    "ps_y": ("psum", [D, 512], "float32"),
-    "ps_sp": ("psum", [D, 512], "float32"),
-    "ps_q": ("psum", [D, 512], "float32"),
-}
-SEMAPHORES = (["ld_m", "ld_q", "fill", "id1", "id2", "sent1", "sent2",
-               "add_y", "cp_y", "mm_sp", "cp_sp", "mm_q", "cp_q", "st_p", "st_q"]
-              + ["a1_%d" % j for j in range(len(_Q[0]))] + ["a2_%d" % u for u in range(len(_Q))])
+    return [sorted(grp, key=topo.chip) for grp in groups]
 
 
 def _send(g, core, topo, dests, ap, remote_sem, local_sem):
@@ -78,74 +54,85 @@ def _send(g, core, topo, dests, ap, remote_sem, local_sem):
 
 
 def rank_program(g, core, T, topo):
-    if T.rank_of(core) is None:
+    me = T.rank_of(core)
+    if me is None:
         return
     S = T.sem
-    quads = _quads(list(T.cores), topo)
-    k = [x for x, qd in enumerate(quads) if core in qd][0]
-    quad = quads[k]
-    pos, na, nb = quad.index(core), len(quad), len(quads)
-    trio = [qd[pos] for qd in quads]
-    ident = T.iq[:, 0:D]
+    groups = _groups(list(T.cores), topo)
+    grp = [x for x in groups if core in x][0]
+    k, n = grp.index(core), len(grp)
+    plane = [x for x in groups if x is not grp and topo.same_plane(x[0], core)][0]
+    partner = [x for x in groups if x is not grp and x is not plane and topo.host(x[0]) == topo.host(core)][0]
+    far = [x for x in groups if x is not grp and x is not plane and x is not partner][0]
 
-    def raw(j):
+    def raw(c):
+        j = T.rank_of(c)
         return T.raw[:, j * D:(j + 1) * D]
 
-    def gs(u):
-        return T.gs[:, u * D:(u + 1) * D]
+    def gs(c):
+        j = T.rank_of(c)
+        return T.gs[:, j * D:(j + 1) * D]
 
-    g.sync.dma_start(raw(pos), T.mt[:, :]).then_inc(S.ld_m, 16)
-    g.sync.dma_start(T.iq[:, D:D + R], T.q[:, :]).then_inc(S.ld_q, 16)
+    def sem(letter, c):
+        return S["%s_%d" % (letter, T.rank_of(c))]
 
-    g.vector.memset(T.idsrc[:, :], 0.0).then_inc(S.fill, 1)
-    g.vector.wait_ge(S.fill, 1)
-    g.vector.memset(T.idsrc[:, 0:1], 1.0).then_inc(S.fill, 1)
-    g.scalar.wait_ge(S.fill, 2)
-    g.scalar.dma_start(T.iddram[:, :], T.idsrc[:, :]).then_inc(S.id1, 16)
-    g.scalar.wait_ge(S.id1, 16)
-    g.scalar.dma_start(ident, T.iddram[0:D, :]).then_inc(S.id2, 16)
+    g.sync.dma_start(raw(core), T.mt[:, :]).then_inc(S.ld_m, 16)
+    g.scalar.dma_start(T.q_sb[:, :], T.q[:, :]).then_inc(S.ld_q, 16)
+    g.vector.memset(T.ones[:, :], 1.0).then_inc(S.fill, 1)
 
     g.wait_ge(S.ld_m, 16)
-    e1 = _send(g, core, topo, [quad[(pos + t) % na] for t in range(1, na)], raw(pos), S["a1_%d" % pos], S.sent1)
+    ne = _send(g, core, topo, [grp[(k + t) % n] for t in range(1, n)] + [far[(k + t) % n] for t in range(n)],
+               raw(core), sem("a", core), S.sent)
+
+    g.wait_ge(S.fill, 1)
+    g.affine_select(T.ident[:, :], T.ones[:, :], [[-1, D]], AluOpType.is_equal, 0.0, 0, 1).then_inc(S.made_i, 1)
 
     g.vector.wait_ge(S.ld_m, 16)
-    acc = raw(pos)
-    for t in range(1, na):
-        j = (pos - t) % na
-        g.vector.wait_ge(S["a1_%d" % j], e1)
+    acc = raw(core)
+    for t in range(1, n):
+        c = grp[(k - t) % n]
+        g.vector.wait_ge(sem("a", c), ne)
         if t > 1:
             g.vector.wait_ge(S.add_y, t - 1)
-        if t < na - 1:
+        if t < n - 1:
             out = T.ps_y[:, (t - 1) * D:t * D]
-            g.vector.tensor_tensor(out, acc, raw(j), AluOpType.add).then_inc(S.add_y, 1)
+            g.vector.tensor_tensor(out, acc, raw(c), AluOpType.add).then_inc(S.add_y, 1)
             acc = out
         else:
-            g.vector.tensor_tensor(gs(k), acc, raw(j), AluOpType.add).then_inc(S.cp_y, 1)
+            g.vector.tensor_tensor(gs(core), acc, raw(c), AluOpType.add).then_inc(S.cp_y, 1)
 
     g.wait_ge(S.cp_y, 1)
-    e2 = _send(g, core, topo, [trio[(k + t) % nb] for t in range(1, nb)], gs(k), S["a2_%d" % k], S.sent2)
+    _send(g, core, topo, [plane[k], partner[k]], gs(core), sem("b", core), S.sent)
 
-    g.tensor.wait_ge(S.id2, 16)
+    todo = ([(S.cp_y, 1, gs(core))]
+            + [(sem("a", far[(k - t) % n]), ne, raw(far[(k - t) % n])) for t in range(n)]
+            + [(sem("b", c), ne, gs(c)) for c in (plane[k], partner[k])])
+    g.tensor.wait_ge(S.made_i, 1)
     g.tensor.wait_ge(S.ld_q, 16)
-    g.tensor.wait_ge(S.cp_y, 1)
-    g.tensor.matmul(T.ps_sp[:, 0:D + R], gs(k), T.iq[:, :], True, False).then_inc(S.mm_sp, 1)
-    for t in range(1, nb):
-        u = (k - t) % nb
-        g.tensor.wait_ge(S["a2_%d" % u], e2)
-        g.tensor.matmul(T.ps_sp[:, 0:D + R], gs(u), T.iq[:, :], False, t == nb - 1).then_inc(S.mm_sp, 1)
-    g.vector.wait_ge(S.mm_sp, nb)
-    g.vector.tensor_copy(T.sp_sb[:, :], T.ps_sp[:, 0:D + R]).then_inc(S.cp_sp, 1)
-    g.sync.wait_ge(S.cp_sp, 1)
-    g.sync.dma_start(T.p[:, :], T.sp_sb[:, D:D + R]).then_inc(S.st_p, 16)
+    for i, (sm, val, x) in enumerate(todo):
+        first, last = i == 0, i == len(todo) - 1
+        g.tensor.wait_ge(sm, val)
+        i_s = g.tensor.matmul(T.ps_s[:, 0:D], x, T.ident[:, :], first, last)
+        i_p = g.tensor.matmul(T.ps_p[:, 0:R], x, T.q_sb[:, :], first, last)
+        if last:
+            i_s.then_inc(S.mm_s, 1)
+            i_p.then_inc(S.mm_p, 1)
 
-    g.tensor.wait_ge(S.cp_sp, 1)
-    g.tensor.matmul(T.ps_q[:, 0:R], T.sp_sb[:, 0:D], T.sp_sb[:, D:D + R], True, True).then_inc(S.mm_q, 1)
+    g.scalar.wait_ge(S.mm_s, 1)
+    g.scalar.activation(T.s_sb[:, :], T.ps_s[:, 0:D], ActivationFunctionType.Copy).then_inc(S.cp_s, 1)
+    g.vector.wait_ge(S.mm_p, 1)
+    g.vector.tensor_copy(T.p_sb[:, :], T.ps_p[:, 0:R]).then_inc(S.cp_p, 1)
+    g.sync.wait_ge(S.cp_p, 1)
+    g.sync.dma_start(T.p[:, :], T.p_sb[:, :]).then_inc(S.st_p, 16)
+
+    g.tensor.wait_ge(S.cp_s, 1)
+    g.tensor.wait_ge(S.cp_p, 1)
+    g.tensor.matmul(T.ps_q[:, 0:R], T.s_sb[:, :], T.p_sb[:, :], True, True).then_inc(S.mm_q, 1)
     g.vector.wait_ge(S.mm_q, 1)
     g.vector.tensor_copy(T.q2_sb[:, :], T.ps_q[:, 0:R]).then_inc(S.cp_q, 1)
     g.scalar.wait_ge(S.cp_q, 1)
     g.scalar.dma_start(T.q2[:, :], T.q2_sb[:, :]).then_inc(S.st_q, 16)
 
-    g.wait_ge(S.sent1, e1)
-    g.wait_ge(S.sent2, e2)
+    g.wait_ge(S.sent, 2 * ne)
     g.wait_ge(S.st_p, 16)
     g.wait_ge(S.st_q, 16)

import comms_topo
from concourse.bass import DstId, RemoteDMATransfer
from concourse.mybir import AluOpType, ActivationFunctionType

CORES = [71, 199, 95, 223, 103, 231, 111, 239, 119, 247, 127, 255]
N = len(CORES)
D = 128
R = 64

SCRATCH = {
    "raw": ("sbuf", [D, N * D], "bfloat16"),
    "gs": ("sbuf", [D, N * D], "bfloat16"),
    "ones": ("sbuf", [D, D], "bfloat16"),
    "ident": ("sbuf", [D, D], "bfloat16"),
    "q_sb": ("sbuf", [D, R], "bfloat16"),
    "s_sb": ("sbuf", [D, D], "bfloat16"),
    "p_sb": ("sbuf", [D, R], "bfloat16"),
    "q2_sb": ("sbuf", [D, R], "bfloat16"),
    "ps_y": ("psum", [D, 512], "float32"),
    "ps_s": ("psum", [D, 512], "float32"),
    "ps_p": ("psum", [D, 512], "float32"),
    "ps_q": ("psum", [D, 512], "float32"),
}
SEMAPHORES = (["ld_m", "ld_q", "fill", "made_i", "sent", "add_y", "cp_y",
               "mm_s", "mm_p", "cp_s", "cp_p", "mm_q", "cp_q", "st_p", "st_q"]
              + ["a_%d" % j for j in range(N)] + ["b_%d" % j for j in range(N)])


def _groups(cores, topo):
    groups = []
    for c in cores:
        for grp in groups:
            if topo.same_plane(grp[0], c) and topo.host(grp[0]) == topo.host(c):
                grp.append(c)
                break
        else:
            groups.append([c])
    return [sorted(grp, key=topo.chip) for grp in groups]


def _send(g, core, topo, dests, ap, remote_sem, local_sem):
    mask = topo.mask(core, dests[0])
    ids = []
    for d in dests:
        assert topo.may_write(core, d)
        mask &= topo.mask(core, d)
        rid, pid = topo.addr(d, core)
        ids.append(DstId(rid=rid, pnc=pid))
    g.remote_dma_fused(
        [RemoteDMATransfer(dst_ids=ids, dma_engine_mask=mask, remote_sem=remote_sem,
                           srcs=[ap], dsts=[ap for _ in dests], alu_op=0)],
        local_sem=local_sem)
    return bin(mask).count("1")


def rank_program(g, core, T, topo):
    me = T.rank_of(core)
    if me is None:
        return
    S = T.sem
    groups = _groups(list(T.cores), topo)
    grp = [x for x in groups if core in x][0]
    k, n = grp.index(core), len(grp)
    plane = [x for x in groups if x is not grp and topo.same_plane(x[0], core)][0]
    partner = [x for x in groups if x is not grp and x is not plane and topo.host(x[0]) == topo.host(core)][0]
    far = [x for x in groups if x is not grp and x is not plane and x is not partner][0]

    def raw(c):
        j = T.rank_of(c)
        return T.raw[:, j * D:(j + 1) * D]

    def gs(c):
        j = T.rank_of(c)
        return T.gs[:, j * D:(j + 1) * D]

    def sem(letter, c):
        return S["%s_%d" % (letter, T.rank_of(c))]

    g.sync.dma_start(raw(core), T.mt[:, :]).then_inc(S.ld_m, 16)
    g.scalar.dma_start(T.q_sb[:, :], T.q[:, :]).then_inc(S.ld_q, 16)
    g.vector.memset(T.ones[:, :], 1.0).then_inc(S.fill, 1)

    g.wait_ge(S.ld_m, 16)
    ne = _send(g, core, topo, [grp[(k + t) % n] for t in range(1, n)] + [far[(k + t) % n] for t in range(n)],
               raw(core), sem("a", core), S.sent)

    g.wait_ge(S.fill, 1)
    g.affine_select(T.ident[:, :], T.ones[:, :], [[-1, D]], AluOpType.is_equal, 0.0, 0, 1).then_inc(S.made_i, 1)

    g.vector.wait_ge(S.ld_m, 16)
    acc = raw(core)
    for t in range(1, n):
        c = grp[(k - t) % n]
        g.vector.wait_ge(sem("a", c), ne)
        if t > 1:
            g.vector.wait_ge(S.add_y, t - 1)
        if t < n - 1:
            out = T.ps_y[:, (t - 1) * D:t * D]
            g.vector.tensor_tensor(out, acc, raw(c), AluOpType.add).then_inc(S.add_y, 1)
            acc = out
        else:
            g.vector.tensor_tensor(gs(core), acc, raw(c), AluOpType.add).then_inc(S.cp_y, 1)

    g.wait_ge(S.cp_y, 1)
    _send(g, core, topo, [plane[k], partner[k]], gs(core), sem("b", core), S.sent)

    todo = ([(S.cp_y, 1, gs(core))]
            + [(sem("a", far[(k - t) % n]), ne, raw(far[(k - t) % n])) for t in range(n)]
            + [(sem("b", c), ne, gs(c)) for c in (plane[k], partner[k])])
    g.tensor.wait_ge(S.made_i, 1)
    g.tensor.wait_ge(S.ld_q, 16)
    for i, (sm, val, x) in enumerate(todo):
        first, last = i == 0, i == len(todo) - 1
        g.tensor.wait_ge(sm, val)
        i_s = g.tensor.matmul(T.ps_s[:, 0:D], x, T.ident[:, :], first, last)
        i_p = g.tensor.matmul(T.ps_p[:, 0:R], x, T.q_sb[:, :], first, last)
        if last:
            i_s.then_inc(S.mm_s, 1)
            i_p.then_inc(S.mm_p, 1)

    g.scalar.wait_ge(S.mm_s, 1)
    g.scalar.activation(T.s_sb[:, :], T.ps_s[:, 0:D], ActivationFunctionType.Copy).then_inc(S.cp_s, 1)
    g.vector.wait_ge(S.mm_p, 1)
    g.vector.tensor_copy(T.p_sb[:, :], T.ps_p[:, 0:R]).then_inc(S.cp_p, 1)
    g.sync.wait_ge(S.cp_p, 1)
    g.sync.dma_start(T.p[:, :], T.p_sb[:, :]).then_inc(S.st_p, 16)

    g.tensor.wait_ge(S.cp_s, 1)
    g.tensor.wait_ge(S.cp_p, 1)
    g.tensor.matmul(T.ps_q[:, 0:R], T.s_sb[:, :], T.p_sb[:, :], True, True).then_inc(S.mm_q, 1)
    g.vector.wait_ge(S.mm_q, 1)
    g.vector.tensor_copy(T.q2_sb[:, :], T.ps_q[:, 0:R]).then_inc(S.cp_q, 1)
    g.scalar.wait_ge(S.cp_q, 1)
    g.scalar.dma_start(T.q2[:, :], T.q2_sb[:, :]).then_inc(S.st_q, 16)

    g.wait_ge(S.sent, 2 * ne)
    g.wait_ge(S.st_p, 16)
    g.wait_ge(S.st_q, 16)
